import numpy as np, ml_dtypes
CORES = [2,6,26,30,66,70,74,78,82,86]
N = 10
import mx_ref
NC, G, MB = 256, 2, 2
C = np.float32(0.037)
BF = ml_dtypes.bfloat16
def cut(t, i, w=512):
    return t[:, w * i:w * i + w]
def tile(rs):
    return np.stack(rs, axis=2).reshape(128, -1).astype(BF)
def layer(w, X):
    out = []
    for i in range(G):
        for t in range(len(X)):
            p = mx_ref.matmul(mx_ref.quantize(cut(w, len(X) * i + t)), X[t])
            z = p if t == 0 else z + p
        out.append(z)
    return out
def act(Z):
    return [np.maximum(s * z, 0) * C for z in Z for s in (1, -1)]
def setup_inputs(rng):
    def f(*shape):
        return mx_ref.flush((rng.standard_normal(shape, dtype=np.float32) * np.exp2(rng.integers(-2, 3, shape[:-1] + (1,)))).astype(BF))
    return {"x": f(N, 128, 4 * NC), "w1": f(N, 128, G * 512), "w2": f(N, 128, 512), "px": f(N, 128, MB * 4 * NC), "pw": f(N, 128, G * 512)}
def setup_inputs_blocks(rng):
    d = setup_inputs(rng)
    for k in ("x", "w1", "w2", "px"): d[k] = mx_ref.spread(d[k], rng, 4)
    for k in ("pw",): d[k] = mx_ref.spread(d[k], rng, 1)
    return d
def setup_inputs_wide(rng):
    d = setup_inputs(rng)
    for k in ("x", "w1", "w2", "px"): d[k] = mx_ref.flush((d[k].astype(np.float32) * np.exp2(rng.integers(-6, 7, (N, 1, 1))).astype(np.float32)).astype(BF))
    return d
def setup_inputs_zeros(rng):
    d = setup_inputs(rng); v = d["x"].reshape(N, 128, -1, 4).copy()
    v[np.broadcast_to((rng.random((N, 1, v.shape[2], 1)) < 0.33), v.shape)] = 0
    d["x"] = v.reshape(d["x"].shape)
    return d
def reference(x, w1, w2, px, pw):
    H = [mx_ref.quantize(tile(act(layer(w1[j], [mx_ref.quantize(x[j])])))) for j in range(N)]
    y = np.zeros((N, 128, N * NC), np.float32)
    for r in range(N):
        qw = mx_ref.quantize(w2[r])
        for j in range(N):
            y[r][:, NC * j:NC * j + NC] = mx_ref.matmul(qw, H[j])
    z = np.full((N, 128, MB * G * NC), np.nan, np.float32)
    for m in range(MB):
        a = mx_ref.quantize(cut(px[N - 1], m, 4 * NC))
        for s in range(N - 1):
            a = mx_ref.quantize(tile(act(layer(pw[s], [a]))))
        Z = layer(pw[N - 1], [a])
        for i in range(G):
            z[N - 1][:, NC * (G * m + i):NC * (G * m + i) + NC] = Z[i]
    return {"y": y, "z": z}

@@ -1,0 +1,302 @@
+import numpy as np
+from concourse.bass import DstId, RemoteDMATransfer
+from concourse.mybir import dt, AluOpType, ActivationFunctionType
+
+N = 10
+NCORES = 96
+PW_ = 128
+CC = float(np.float32(0.037))
+
+RUNS = [
+    [(0, 0, 1), (2, 2, 3), (4, 4, 5), (7, 6, 7), (6, 8, 8)],
+    [(1, 0, 1), (3, 2, 3), (5, 4, 5), (7, 6, 7), (8, 8, 8)],
+    [(0, 0, 1), (2, 2, 3), (4, 4, 5), (6, 6, 8)],
+    [(1, 0, 1), (3, 2, 3), (5, 4, 5), (8, 6, 8)],
+]
+ORDER = {0: [0, 2], 1: [1, 3], 2: [0, 2], 3: [1, 3], 4: [0, 2], 5: [1, 3], 6: [2, 0], 7: [0, 1], 8: [3, 1], 9: [2, 0, 3, 1]}
+EARLY = {0: 0, 1: 0, 2: 0, 3: 0, 4: 1, 5: 1, 6: 2, 7: 2, 8: 3, 9: 5}
+
+SCRATCH = {
+    "xt": ("sbuf", [128, 1024], "bfloat16"),
+    "w1t": ("sbuf", [128, 1024], "bfloat16"),
+    "w2t": ("sbuf", [128, 512], "bfloat16"),
+    "pwt": ("sbuf", [128, 1024], "bfloat16"),
+    "pxt": ("sbuf", [128, 2048], "bfloat16"),
+    "ht": ("sbuf", [128, 1024], "bfloat16"),
+    "ct": ("sbuf", [128, 2048], "bfloat16"),
+    "xc": ("sbuf", [128, 256], "float8_e4m3fn_x4"), "xs": ("sbuf", [128, 256], "uint8"),
+    "w1c": ("sbuf", [128, 256], "float8_e4m3fn_x4"), "w1s": ("sbuf", [128, 256], "uint8"),
+    "w2c": ("sbuf", [128, 128], "float8_e4m3fn_x4"), "w2s": ("sbuf", [128, 128], "uint8"),
+    "wc": ("sbuf", [128, 768], "float8_e4m3fn_x4"), "ws": ("sbuf", [128, 768], "uint8"),
+    "pxc": ("sbuf", [128, 512], "float8_e4m3fn_x4"), "pxs": ("sbuf", [128, 512], "uint8"),
+    "cc": ("sbuf", [128, 512], "float8_e4m3fn_x4"), "cs": ("sbuf", [128, 512], "uint8"),
+    "lc": ("sbuf", [128, 512], "float8_e4m3fn_x4"), "ls": ("sbuf", [128, 512], "uint8"),
+    "hc": ("sbuf", [128, 2560], "float8_e4m3fn_x4"), "hs": ("sbuf", [128, 2560], "uint8"),
+    "ysb": ("sbuf", [128, 2560], "float32"),
+    "zsb": ("sbuf", [128, 1024], "float32"),
+    "pc": ("psum", [128, 2048], "float32"),
+    "py": ("psum", [128, 2048], "float32"),
+}
+SEMAPHORES = (["ld_pw", "ld_x", "ld_w1", "ld_w2", "q_pw", "q_x", "q_w1", "q_w2", "zh0", "zh1", "act_h", "q_h", "sent", "sty", "stz"]
+              + ["ld_p%d" % p for p in range(4)] + ["q_p%d" % p for p in range(4)] + ["ap%d" % p for p in range(4)]
+              + ["aw%d" % s for s in range(N)] + ["ah%d" % j for j in range(N)]
+              + ["%s%d" % (a, k) for a in ("z0_", "z1_", "act", "q") for k in range(4)]
+              + ["%s%d" % (a, k) for a in ("my", "cy") for k in range(5)]
+              + ["zc%d_%d" % (p, i) for p in range(4) for i in range(2)])
+
+
+def layers_of(rank):
+    if rank == N - 1:
+        return [N - 1]
+    own = set()
+    for runs in RUNS:
+        for r, a, b in runs:
+            if r == rank:
+                own |= set(range(a, b + 1))
+    own.add(rank)
+    return sorted(own)
+
+
+def needs(rank, layer):
+    return rank != N - 1 and any(r == rank and a <= layer <= b for runs in RUNS for r, a, b in runs)
+
+
+def bits(m):
+    return bin(m).count("1")
+
+
+def helper_of(core, T, topo):
+    for c in range(NCORES):
+        if (c not in T.cores and topo.chip(c) == topo.chip(core) and topo.die(c) == topo.die(core)
+                and all(topo.may_write(c, d) for d in T.cores)):
+            return c
+    return None
+
+
+def rank_program(g, core, T, topo):
+    rank = T.rank_of(core)
+    cores = T.cores
+    helpers = [helper_of(c, T, topo) for c in cores]
+    chips = []
+    for c in cores:
+        if topo.chip(c) not in chips:
+            chips.append(topo.chip(c))
+    if rank is None and core not in helpers:
+        return
+    sent = [0]
+    mine = topo.chip(core)
+    OFF = 0
+    ALL = 0
+    for c in cores + helpers:
+        if topo.chip(c) != mine:
+            OFF = topo.mask(core, c)
+        elif c != core:
+            ALL = topo.mask(core, c)
+    BULK = ALL & ~OFF
+
+    def ids(dsts):
+        out = []
+        for d in dsts:
+            rid, pid, _s = topo.addr(d)
+            out.append(DstId(rid=rid, pnc=pid))
+        return out
+
+    def send(dsts, sc, ss, dc, ds, sem, mask):
+        for a, b in ((sc.bitcast(dt.uint8), dc.bitcast(dt.uint8)), (ss, ds)):
+            if len(dsts) == 1:
+                rid, pid, _s = topo.addr(dsts[0])
+                g.remote_dma(b, a, sem, T.sem.sent, pid, rid, mask)
+            else:
+                g.remote_dma_fused([RemoteDMATransfer(dst_ids=ids(dsts), dma_engine_mask=mask, remote_sem=sem,
+                                                      srcs=[a], dsts=[b for _ in dsts])], local_sem=T.sem.sent)
+            sent[0] += bits(mask)
+
+    def send_h(j, dsts, mask):
+        a, b = 256 * j, 256 * j + 256
+        send(dsts, T.hc[:, a:b], T.hs[:, a:b], T.hc[:, a:b], T.hs[:, a:b], T.sem["ah%d" % j], mask)
+
+    if rank is None:
+        own = helpers.index(core)
+        i = chips.index(mine)
+        nc = len(chips)
+
+        def at_chip(k):
+            for j, c in enumerate(cores):
+                if topo.chip(c) == chips[k] and topo.die(c) == topo.die(core):
+                    return j
+        here = [c for c in cores if topo.chip(c) == mine]
+        g.wait_ge(T.sem["ah%d" % own], 16)
+        for p in range(1, nc):
+            send_h(own, [helpers[at_chip((i + p) % nc)]], OFF)
+        for p in range(1, nc):
+            j = at_chip((i - p) % nc)
+            g.wait_ge(T.sem["ah%d" % j], 16)
+            send_h(j, here, BULK)
+        g.wait_ge(T.sem.sent, sent[0])
+        return
+
+    last = rank == N - 1
+    partner = [c for c in cores if c != core and topo.chip(c) == mine][0]
+    V, S, P, Y = g.vector, g.scalar, g.tensor, g.sync
+    RELU, COPY = ActivationFunctionType.Relu, ActivationFunctionType.Copy
+    held = layers_of(rank)
+    hs0 = 256 * rank
+
+    if last:
+        for p in range(4):
+            o = 1024 * (p % 2) + 512 * (p // 2)
+            Y.dma_start(T.pxt[:, 512 * p:512 * p + 512], T.px[:, o:o + 512]).then_inc(T.sem["ld_p%d" % p], 16)
+        S.wait_ge(T.sem.ld_p1, 16)
+        S.dma_start(T.xt[:], T.x[:]).then_inc(T.sem.ld_x, 16)
+        S.dma_start(T.w1t[:], T.w1[:]).then_inc(T.sem.ld_w1, 16)
+        S.dma_start(T.w2t[:], T.w2[:]).then_inc(T.sem.ld_w2, 16)
+        S.dma_start(T.pwt[:], T.pw[:]).then_inc(T.sem.ld_pw, 16)
+    else:
+        Y.dma_start(T.pwt[:], T.pw[:]).then_inc(T.sem.ld_pw, 16)
+        S.dma_start(T.xt[:], T.x[:]).then_inc(T.sem.ld_x, 16)
+        Y.dma_start(T.w1t[:], T.w1[:]).then_inc(T.sem.ld_w1, 16)
+        S.dma_start(T.w2t[:], T.w2[:]).then_inc(T.sem.ld_w2, 16)
+
+    def quant_pw():
+        k = held.index(rank)
+        V.wait_ge(T.sem.ld_pw, 16)
+        V.quantize_mx(T.wc[:, 256 * k:256 * k + 256], T.ws[:, 256 * k:256 * k + 256], T.pwt[:]).then_inc(T.sem.q_pw, 1)
+
+    def acts(z0, z1, t, a, n, s0, s1, done):
+        S.wait_ge(s0, 1)
+        S.activation(t[:, a:a + 4 * n:4], z0, RELU, scale=CC).then_inc(done, 1)
+        S.activation(t[:, a + 1:a + 4 * n:4], z0, RELU, scale=-CC).then_inc(done, 1)
+        V.wait_ge(s1, 1)
+        V.tensor_scalar(t[:, a + 2:a + 4 * n:4], z1, CC, 0.0, AluOpType.mult, AluOpType.max).then_inc(done, 1)
+        V.tensor_scalar(t[:, a + 3:a + 4 * n:4], z1, -CC, 0.0, AluOpType.mult, AluOpType.max).then_inc(done, 1)
+        V.wait_ge(done, 4)
+
+    if last:
+        for p in range(4):
+            V.wait_ge(T.sem["ld_p%d" % p], 16)
+            c = slice(PW_ * p, PW_ * p + PW_)
+            V.quantize_mx(T.pxc[:, c], T.pxs[:, c], T.pxt[:, 512 * p:512 * p + 512]).then_inc(T.sem["q_p%d" % p], 1)
+            g.wait_ge(T.sem["q_p%d" % p], 1)
+            send([cores[RUNS[p][0][0]]], T.pxc[:, c], T.pxs[:, c], T.lc[:, c], T.ls[:, c], T.sem["ap%d" % p], OFF)
+    else:
+        quant_pw()
+        k = held.index(rank)
+        g.wait_ge(T.sem.q_pw, 1)
+        groups = {}
+        for r in range(N - 1):
+            if r != rank and needs(r, rank):
+                groups.setdefault(layers_of(r).index(rank), []).append(cores[r])
+        for slot, dsts in groups.items():
+            send(dsts, T.wc[:, 256 * k:256 * k + 256], T.ws[:, 256 * k:256 * k + 256],
+                 T.wc[:, 256 * slot:256 * slot + 256], T.ws[:, 256 * slot:256 * slot + 256], T.sem["aw%d" % rank], OFF)
+
+    V.wait_ge(T.sem.ld_x, 16)
+    V.quantize_mx(T.xc[:], T.xs[:], T.xt[:]).then_inc(T.sem.q_x, 1)
+    V.wait_ge(T.sem.ld_w1, 16)
+    V.quantize_mx(T.w1c[:], T.w1s[:], T.w1t[:]).then_inc(T.sem.q_w1, 1)
+    P.wait_ge(T.sem.q_x, 1)
+    P.wait_ge(T.sem.q_w1, 1)
+    zh = [T.py[:, 0:256], T.py[:, 512:768]]
+    for i in range(2):
+        P.matmul_mx(zh[i], T.w1c[:, 128 * i:128 * i + 128], T.w1s[:, 128 * i:128 * i + 128], T.xc[:], T.xs[:],
+                    True, True).then_inc(T.sem["zh%d" % i], 1)
+    acts(zh[0], zh[1], T.ht, 0, 256, T.sem.zh0, T.sem.zh1, T.sem.act_h)
+    V.quantize_mx(T.hc[:, hs0:hs0 + 256], T.hs[:, hs0:hs0 + 256], T.ht[:]).then_inc(T.sem.q_h, 1)
+    g.wait_ge(T.sem.q_h, 1)
+    send_h(rank, [helpers[rank], partner], BULK)
+    V.wait_ge(T.sem.ld_w2, 16)
+    V.quantize_mx(T.w2c[:], T.w2s[:], T.w2t[:]).then_inc(T.sem.q_w2, 1)
+    if last:
+        quant_pw()
+
+    P.wait_ge(T.sem.q_h, 1)
+    P.wait_ge(T.sem.q_w2, 1)
+    ci = chips.index(mine)
+    order = [chips[(ci - p) % len(chips)] for p in range(len(chips))]
+
+    def y_group(q):
+        js = [j for j in range(N) if topo.chip(cores[j]) == order[q]]
+        a = 256 * js[0]
+        b = (2 + q) % 4
+        for j in js:
+            if j != rank:
+                P.wait_ge(T.sem["ah%d" % j], 16)
+        if q == 4:
+            P.wait_ge(T.sem.cy0, 1)
+        bank = T.py[:, 512 * b:512 * b + 512]
+        P.matmul_mx(bank, T.w2c[:], T.w2s[:], T.hc[:, a:a + 512], T.hs[:, a:a + 512], True, True).then_inc(T.sem["my%d" % q], 1)
+        if q % 2 == 0:
+            S.wait_ge(T.sem["my%d" % q], 1)
+            S.activation(T.ysb[:, a:a + 512], bank, COPY).then_inc(T.sem["cy%d" % q], 1)
+        else:
+            V.wait_ge(T.sem["my%d" % q], 1)
+            V.tensor_copy(T.ysb[:, a:a + 512], bank).then_inc(T.sem["cy%d" % q], 1)
+        Y.wait_ge(T.sem["cy%d" % q], 1)
+        Y.dma_start(T.y[:, a:a + 512], T.ysb[:, a:a + 512]).then_inc(T.sem.sty, 16)
+
+    for q in range(EARLY[rank]):
+        y_group(q)
+
+    n = [0]
+
+    def layer(s, mc, ms, wait, wn):
+        k = n[0]
+        sl = held.index(s)
+        if s == rank:
+            P.wait_ge(T.sem.q_pw, 1)
+        else:
+            P.wait_ge(T.sem["aw%d" % s], 16)
+        P.wait_ge(wait, wn)
+        out = []
+        for i in range(2):
+            b = 2 * (k % 2) + i
+            z = T.pc[:, 512 * b:512 * b + PW_]
+            w = slice(256 * sl + 128 * i, 256 * sl + 128 * i + 128)
+            P.matmul_mx(z, T.wc[:, w], T.ws[:, w], mc, ms, True, True).then_inc(T.sem["z%d_%d" % (i, k)], 1)
+            out.append(z)
+        n[0] += 1
+        return k, out
+
+    for p in ORDER[rank]:
+        c = slice(PW_ * p, PW_ * p + PW_)
+        path = [N - 1] + [r for r, _a, _b in RUNS[p]] + [N - 1]
+        at = len(path) - 1 if last else path.index(rank, 1)
+        src = cores[path[at - 1]]
+        mc, ms, wait, wn = T.lc[:, c], T.ls[:, c], T.sem["ap%d" % p], 2 * bits(topo.mask(src, core))
+        if last:
+            if n[0] >= 2:
+                for i in range(2):
+                    P.wait_ge(T.sem["zc%d_%d" % (ORDER[rank][n[0] - 2], i)], 1)
+            k, Z = layer(N - 1, mc, ms, wait, wn)
+            for i in range(2):
+                o = 256 * (2 * (p % 2) + i) + PW_ * (p // 2)
+                zs = T.zsb[:, o:o + PW_]
+                done = T.sem["zc%d_%d" % (p, i)]
+                if i == 0:
+                    S.wait_ge(T.sem["z0_%d" % k], 1)
+                    S.activation(zs, Z[0], COPY).then_inc(done, 1)
+                else:
+                    V.wait_ge(T.sem["z1_%d" % k], 1)
+                    V.tensor_copy(zs, Z[1]).then_inc(done, 1)
+                Q = S if i == 0 else Y
+                Q.wait_ge(done, 1)
+                Q.dma_start(T.z[:, o:o + PW_], zs).then_inc(T.sem.stz, 16)
+            continue
+        _r, s0, s1 = RUNS[p][at - 1]
+        dst = cores[path[at + 1]]
+        for s in range(s0, s1 + 1):
+            k, Z = layer(s, mc, ms, wait, wn)
+            acts(Z[0], Z[1], T.ct, 512 * k, PW_, T.sem["z0_%d" % k], T.sem["z1_%d" % k], T.sem["act%d" % k])
+            o = slice(PW_ * k, PW_ * k + PW_)
+            mc, ms, wait, wn = T.cc[:, o], T.cs[:, o], T.sem["q%d" % k], 1
+            V.quantize_mx(mc, ms, T.ct[:, 512 * k:512 * k + 512]).then_inc(wait, 1)
+        g.wait_ge(wait, 1)
+        send([dst], mc, ms, T.lc[:, c], T.ls[:, c], T.sem["ap%d" % p], topo.mask(core, dst))
+
+    for q in range(EARLY[rank], 5):
+        y_group(q)
+
+    Y.wait_ge(T.sem.sty, 80)
+    if last:
+        Y.wait_ge(T.sem.stz, 128)
+    g.wait_ge(T.sem.sent, sent[0])

@@ -8,13 +8,13 @@ PW_ = 128
 CC = float(np.float32(0.037))
 
 RUNS = [
-    [(0, 0, 1), (2, 2, 3), (4, 4, 5), (7, 6, 7), (6, 8, 8)],
-    [(1, 0, 1), (3, 2, 3), (5, 4, 5), (7, 6, 7), (8, 8, 8)],
-    [(0, 0, 1), (2, 2, 3), (4, 4, 5), (6, 6, 8)],
-    [(1, 0, 1), (3, 2, 3), (5, 4, 5), (8, 6, 8)],
+    [(0, 0, 1), (2, 2, 3), (3, 4, 5), (7, 6, 7), (6, 8, 8)],
+    [(1, 0, 1), (5, 2, 3), (4, 4, 5), (7, 6, 7), (8, 8, 8)],
+    [(0, 0, 1), (2, 2, 3), (3, 4, 5), (6, 6, 8)],
+    [(1, 0, 1), (5, 2, 3), (4, 4, 5), (8, 6, 8)],
 ]
-ORDER = {0: [0, 2], 1: [1, 3], 2: [0, 2], 3: [1, 3], 4: [0, 2], 5: [1, 3], 6: [2, 0], 7: [0, 1], 8: [3, 1], 9: [2, 0, 3, 1]}
-EARLY = {0: 0, 1: 0, 2: 0, 3: 0, 4: 1, 5: 1, 6: 2, 7: 2, 8: 3, 9: 5}
+ORDER = {0: [0, 2], 1: [1, 3], 2: [0, 2], 3: [0, 2], 4: [1, 3], 5: [1, 3], 6: [2, 0], 7: [0, 1], 8: [3, 1], 9: [2, 3, 0, 1]}
+EARLY = {0: 0, 1: 0, 2: 0, 3: 0, 4: 0, 5: 0, 6: 3, 7: 1, 8: 4, 9: 5}
 
 SCRATCH = {
     "xt": ("sbuf", [128, 1024], "bfloat16"),
@@ -27,7 +27,7 @@ SCRATCH = {
     "xc": ("sbuf", [128, 256], "float8_e4m3fn_x4"), "xs": ("sbuf", [128, 256], "uint8"),
     "w1c": ("sbuf", [128, 256], "float8_e4m3fn_x4"), "w1s": ("sbuf", [128, 256], "uint8"),
     "w2c": ("sbuf", [128, 128], "float8_e4m3fn_x4"), "w2s": ("sbuf", [128, 128], "uint8"),
-    "wc": ("sbuf", [128, 768], "float8_e4m3fn_x4"), "ws": ("sbuf", [128, 768], "uint8"),
+    "wc": ("sbuf", [128, 1024], "float8_e4m3fn_x4"), "ws": ("sbuf", [128, 1024], "uint8"),
     "pxc": ("sbuf", [128, 512], "float8_e4m3fn_x4"), "pxs": ("sbuf", [128, 512], "uint8"),
     "cc": ("sbuf", [128, 512], "float8_e4m3fn_x4"), "cs": ("sbuf", [128, 512], "uint8"),
     "lc": ("sbuf", [128, 512], "float8_e4m3fn_x4"), "ls": ("sbuf", [128, 512], "uint8"),
@@ -45,49 +45,42 @@ SEMAPHORES = (["ld_pw", "ld_x", "ld_w1", "ld_w2", "q_pw", "q_x", "q_w1", "q_w2",
               + ["zc%d_%d" % (p, i) for p in range(4) for i in range(2)])
 
 
-def layers_of(rank):
-    if rank == N - 1:
-        return [N - 1]
-    own = set()
-    for runs in RUNS:
-        for r, a, b in runs:
-            if r == rank:
-                own |= set(range(a, b + 1))
-    own.add(rank)
-    return sorted(own)
-
-
 def needs(rank, layer):
-    return rank != N - 1 and any(r == rank and a <= layer <= b for runs in RUNS for r, a, b in runs)
+    return (rank == layer if rank == N - 1 else
+            any(r == rank and a <= layer <= b for runs in RUNS for r, a, b in runs))
+
+
+def slot_of(rank, layer):
+    return layer % 3 if needs(rank, layer) else 3
 
 
 def bits(m):
     return bin(m).count("1")
 
 
-def helper_of(core, T, topo):
-    for c in range(NCORES):
-        if (c not in T.cores and topo.chip(c) == topo.chip(core) and topo.die(c) == topo.die(core)
-                and all(topo.may_write(c, d) for d in T.cores)):
-            return c
-    return None
+def helpers_of(core, T, topo):
+    near = [c for c in range(NCORES) if c not in T.cores and topo.chip(c) == topo.chip(core) and topo.die(c) == topo.die(core)]
+    out = [c for c in near if all(topo.may_write(c, d) for d in T.cores)][0]
+    return out, [c for c in near if c != out][0]
 
 
 def rank_program(g, core, T, topo):
     rank = T.rank_of(core)
     cores = T.cores
-    helpers = [helper_of(c, T, topo) for c in cores]
+    pairs = [helpers_of(c, T, topo) for c in cores]
+    helpers = [a for a, _b in pairs]
+    takers = [b for _a, b in pairs]
     chips = []
     for c in cores:
         if topo.chip(c) not in chips:
             chips.append(topo.chip(c))
-    if rank is None and core not in helpers:
+    if rank is None and core not in helpers + takers:
         return
     sent = [0]
     mine = topo.chip(core)
     OFF = 0
     ALL = 0
-    for c in cores + helpers:
+    for c in cores + helpers + takers:
         if topo.chip(c) != mine:
             OFF = topo.mask(core, c)
         elif c != core:
@@ -116,7 +109,6 @@ def rank_program(g, core, T, topo):
         send(dsts, T.hc[:, a:b], T.hs[:, a:b], T.hc[:, a:b], T.hs[:, a:b], T.sem["ah%d" % j], mask)
 
     if rank is None:
-        own = helpers.index(core)
         i = chips.index(mine)
         nc = len(chips)
 
@@ -125,40 +117,42 @@ def rank_program(g, core, T, topo):
                 if topo.chip(c) == chips[k] and topo.die(c) == topo.die(core):
                     return j
         here = [c for c in cores if topo.chip(c) == mine]
-        g.wait_ge(T.sem["ah%d" % own], 16)
-        for p in range(1, nc):
-            send_h(own, [helpers[at_chip((i + p) % nc)]], OFF)
-        for p in range(1, nc):
-            j = at_chip((i - p) % nc)
-            g.wait_ge(T.sem["ah%d" % j], 16)
-            send_h(j, here, BULK)
+        own = at_chip(i)
+        g.wait_ge(T.sem["ah%d" % own], 2 * bits(BULK))
+        if core in helpers:
+            for p in range(1, nc):
+                send_h(own, [takers[at_chip((i + p) % nc)]], OFF)
+        else:
+            send_h(own, [c for c in here if c != cores[own]], ALL)
+            for p in range(1, nc):
+                j = at_chip((i - p) % nc)
+                g.wait_ge(T.sem["ah%d" % j], 2 * bits(OFF))
+                send_h(j, here, ALL)
         g.wait_ge(T.sem.sent, sent[0])
         return
 
     last = rank == N - 1
-    partner = [c for c in cores if c != core and topo.chip(c) == mine][0]
     V, S, P, Y = g.vector, g.scalar, g.tensor, g.sync
     RELU, COPY = ActivationFunctionType.Relu, ActivationFunctionType.Copy
-    held = layers_of(rank)
     hs0 = 256 * rank
 
     if last:
         for p in range(4):
             o = 1024 * (p % 2) + 512 * (p // 2)
             Y.dma_start(T.pxt[:, 512 * p:512 * p + 512], T.px[:, o:o + 512]).then_inc(T.sem["ld_p%d" % p], 16)
-        S.wait_ge(T.sem.ld_p1, 16)
-        S.dma_start(T.xt[:], T.x[:]).then_inc(T.sem.ld_x, 16)
-        S.dma_start(T.w1t[:], T.w1[:]).then_inc(T.sem.ld_w1, 16)
-        S.dma_start(T.w2t[:], T.w2[:]).then_inc(T.sem.ld_w2, 16)
-        S.dma_start(T.pwt[:], T.pw[:]).then_inc(T.sem.ld_pw, 16)
+        Y.dma_start(T.xt[:], T.x[:]).then_inc(T.sem.ld_x, 16)
+        Y.dma_start(T.w1t[:], T.w1[:]).then_inc(T.sem.ld_w1, 16)
+        Y.wait_ge(T.sem.q_h, 1)
+        Y.dma_start(T.w2t[:], T.w2[:]).then_inc(T.sem.ld_w2, 16)
+        Y.dma_start(T.pwt[:], T.pw[:]).then_inc(T.sem.ld_pw, 16)
     else:
         Y.dma_start(T.pwt[:], T.pw[:]).then_inc(T.sem.ld_pw, 16)
-        S.dma_start(T.xt[:], T.x[:]).then_inc(T.sem.ld_x, 16)
+        Y.dma_start(T.xt[:], T.x[:]).then_inc(T.sem.ld_x, 16)
         Y.dma_start(T.w1t[:], T.w1[:]).then_inc(T.sem.ld_w1, 16)
-        S.dma_start(T.w2t[:], T.w2[:]).then_inc(T.sem.ld_w2, 16)
+        Y.dma_start(T.w2t[:], T.w2[:]).then_inc(T.sem.ld_w2, 16)
 
     def quant_pw():
-        k = held.index(rank)
+        k = slot_of(rank, rank)
         V.wait_ge(T.sem.ld_pw, 16)
         V.quantize_mx(T.wc[:, 256 * k:256 * k + 256], T.ws[:, 256 * k:256 * k + 256], T.pwt[:]).then_inc(T.sem.q_pw, 1)
 
@@ -180,15 +174,11 @@ def rank_program(g, core, T, topo):
             send([cores[RUNS[p][0][0]]], T.pxc[:, c], T.pxs[:, c], T.lc[:, c], T.ls[:, c], T.sem["ap%d" % p], OFF)
     else:
         quant_pw()
-        k = held.index(rank)
+        k = 256 * slot_of(rank, rank)
+        k2 = 256 * (rank % 3)
         g.wait_ge(T.sem.q_pw, 1)
-        groups = {}
-        for r in range(N - 1):
-            if r != rank and needs(r, rank):
-                groups.setdefault(layers_of(r).index(rank), []).append(cores[r])
-        for slot, dsts in groups.items():
-            send(dsts, T.wc[:, 256 * k:256 * k + 256], T.ws[:, 256 * k:256 * k + 256],
-                 T.wc[:, 256 * slot:256 * slot + 256], T.ws[:, 256 * slot:256 * slot + 256], T.sem["aw%d" % rank], OFF)
+        dsts = [cores[r] for r in range(N) if r != rank and needs(r, rank)]
+        send(dsts, T.wc[:, k:k + 256], T.ws[:, k:k + 256], T.wc[:, k2:k2 + 256], T.ws[:, k2:k2 + 256], T.sem["aw%d" % rank], OFF)
 
     V.wait_ge(T.sem.ld_x, 16)
     V.quantize_mx(T.xc[:], T.xs[:], T.xt[:]).then_inc(T.sem.q_x, 1)
@@ -203,7 +193,7 @@ def rank_program(g, core, T, topo):
     acts(zh[0], zh[1], T.ht, 0, 256, T.sem.zh0, T.sem.zh1, T.sem.act_h)
     V.quantize_mx(T.hc[:, hs0:hs0 + 256], T.hs[:, hs0:hs0 + 256], T.ht[:]).then_inc(T.sem.q_h, 1)
     g.wait_ge(T.sem.q_h, 1)
-    send_h(rank, [helpers[rank], partner], BULK)
+    send_h(rank, [helpers[rank], takers[rank]], BULK)
     V.wait_ge(T.sem.ld_w2, 16)
     V.quantize_mx(T.w2c[:], T.w2s[:], T.w2t[:]).then_inc(T.sem.q_w2, 1)
     if last:
@@ -220,7 +210,7 @@ def rank_program(g, core, T, topo):
         b = (2 + q) % 4
         for j in js:
             if j != rank:
-                P.wait_ge(T.sem["ah%d" % j], 16)
+                P.wait_ge(T.sem["ah%d" % j], 2 * bits(ALL))
         if q == 4:
             P.wait_ge(T.sem.cy0, 1)
         bank = T.py[:, 512 * b:512 * b + 512]
@@ -241,11 +231,11 @@ def rank_program(g, core, T, topo):
 
     def layer(s, mc, ms, wait, wn):
         k = n[0]
-        sl = held.index(s)
+        sl = slot_of(rank, s)
         if s == rank:
             P.wait_ge(T.sem.q_pw, 1)
         else:
-            P.wait_ge(T.sem["aw%d" % s], 16)
+            P.wait_ge(T.sem["aw%d" % s], 2 * bits(OFF))
         P.wait_ge(wait, wn)
         out = []
         for i in range(2):
@@ -261,8 +251,7 @@ def rank_program(g, core, T, topo):
         c = slice(PW_ * p, PW_ * p + PW_)
         path = [N - 1] + [r for r, _a, _b in RUNS[p]] + [N - 1]
         at = len(path) - 1 if last else path.index(rank, 1)
-        src = cores[path[at - 1]]
-        mc, ms, wait, wn = T.lc[:, c], T.ls[:, c], T.sem["ap%d" % p], 2 * bits(topo.mask(src, core))
+        mc, ms, wait, wn = T.lc[:, c], T.ls[:, c], T.sem["ap%d" % p], 2 * bits(topo.mask(cores[path[at - 1]], core))
         if last:
             if n[0] >= 2:
                 for i in range(2):
@@ -283,16 +272,18 @@ def rank_program(g, core, T, topo):
                 Q.dma_start(T.z[:, o:o + PW_], zs).then_inc(T.sem.stz, 16)
             continue
         _r, s0, s1 = RUNS[p][at - 1]
-        dst = cores[path[at + 1]]
         for s in range(s0, s1 + 1):
             k, Z = layer(s, mc, ms, wait, wn)
             acts(Z[0], Z[1], T.ct, 512 * k, PW_, T.sem["z0_%d" % k], T.sem["z1_%d" % k], T.sem["act%d" % k])
             o = slice(PW_ * k, PW_ * k + PW_)
             mc, ms, wait, wn = T.cc[:, o], T.cs[:, o], T.sem["q%d" % k], 1
             V.quantize_mx(mc, ms, T.ct[:, 512 * k:512 * k + 512]).then_inc(wait, 1)
+        dst = cores[path[at + 1]]
         g.wait_ge(wait, 1)
         send([dst], mc, ms, T.lc[:, c], T.ls[:, c], T.sem["ap%d" % p], topo.mask(core, dst))
 
+    if not last:
+        Y.wait_ge(T.sem.sent, sent[0])
     for q in range(EARLY[rank], 5):
         y_group(q)
 

import numpy as np
from concourse.bass import DstId, RemoteDMATransfer
from concourse.mybir import dt, AluOpType, ActivationFunctionType

N = 10
NCORES = 96
PW_ = 128
CC = float(np.float32(0.037))

RUNS = [
    [(0, 0, 1), (2, 2, 3), (3, 4, 5), (7, 6, 7), (6, 8, 8)],
    [(1, 0, 1), (5, 2, 3), (4, 4, 5), (7, 6, 7), (8, 8, 8)],
    [(0, 0, 1), (2, 2, 3), (3, 4, 5), (6, 6, 8)],
    [(1, 0, 1), (5, 2, 3), (4, 4, 5), (8, 6, 8)],
]
ORDER = {0: [0, 2], 1: [1, 3], 2: [0, 2], 3: [0, 2], 4: [1, 3], 5: [1, 3], 6: [2, 0], 7: [0, 1], 8: [3, 1], 9: [2, 3, 0, 1]}
EARLY = {0: 0, 1: 0, 2: 0, 3: 0, 4: 0, 5: 0, 6: 3, 7: 1, 8: 4, 9: 5}

SCRATCH = {
    "xt": ("sbuf", [128, 1024], "bfloat16"),
    "w1t": ("sbuf", [128, 1024], "bfloat16"),
    "w2t": ("sbuf", [128, 512], "bfloat16"),
    "pwt": ("sbuf", [128, 1024], "bfloat16"),
    "pxt": ("sbuf", [128, 2048], "bfloat16"),
    "ht": ("sbuf", [128, 1024], "bfloat16"),
    "ct": ("sbuf", [128, 2048], "bfloat16"),
    "xc": ("sbuf", [128, 256], "float8_e4m3fn_x4"), "xs": ("sbuf", [128, 256], "uint8"),
    "w1c": ("sbuf", [128, 256], "float8_e4m3fn_x4"), "w1s": ("sbuf", [128, 256], "uint8"),
    "w2c": ("sbuf", [128, 128], "float8_e4m3fn_x4"), "w2s": ("sbuf", [128, 128], "uint8"),
    "wc": ("sbuf", [128, 1024], "float8_e4m3fn_x4"), "ws": ("sbuf", [128, 1024], "uint8"),
    "pxc": ("sbuf", [128, 512], "float8_e4m3fn_x4"), "pxs": ("sbuf", [128, 512], "uint8"),
    "cc": ("sbuf", [128, 512], "float8_e4m3fn_x4"), "cs": ("sbuf", [128, 512], "uint8"),
    "lc": ("sbuf", [128, 512], "float8_e4m3fn_x4"), "ls": ("sbuf", [128, 512], "uint8"),
    "hc": ("sbuf", [128, 2560], "float8_e4m3fn_x4"), "hs": ("sbuf", [128, 2560], "uint8"),
    "ysb": ("sbuf", [128, 2560], "float32"),
    "zsb": ("sbuf", [128, 1024], "float32"),
    "pc": ("psum", [128, 2048], "float32"),
    "py": ("psum", [128, 2048], "float32"),
}
SEMAPHORES = (["ld_pw", "ld_x", "ld_w1", "ld_w2", "q_pw", "q_x", "q_w1", "q_w2", "zh0", "zh1", "act_h", "q_h", "sent", "sty", "stz"]
              + ["ld_p%d" % p for p in range(4)] + ["q_p%d" % p for p in range(4)] + ["ap%d" % p for p in range(4)]
              + ["aw%d" % s for s in range(N)] + ["ah%d" % j for j in range(N)]
              + ["%s%d" % (a, k) for a in ("z0_", "z1_", "act", "q") for k in range(4)]
              + ["%s%d" % (a, k) for a in ("my", "cy") for k in range(5)]
              + ["zc%d_%d" % (p, i) for p in range(4) for i in range(2)])


def needs(rank, layer):
    return (rank == layer if rank == N - 1 else
            any(r == rank and a <= layer <= b for runs in RUNS for r, a, b in runs))


def slot_of(rank, layer):
    return layer % 3 if needs(rank, layer) else 3


def bits(m):
    return bin(m).count("1")


def helpers_of(core, T, topo):
    near = [c for c in range(NCORES) if c not in T.cores and topo.chip(c) == topo.chip(core) and topo.die(c) == topo.die(core)]
    out = [c for c in near if all(topo.may_write(c, d) for d in T.cores)][0]
    return out, [c for c in near if c != out][0]


def rank_program(g, core, T, topo):
    rank = T.rank_of(core)
    cores = T.cores
    pairs = [helpers_of(c, T, topo) for c in cores]
    helpers = [a for a, _b in pairs]
    takers = [b for _a, b in pairs]
    chips = []
    for c in cores:
        if topo.chip(c) not in chips:
            chips.append(topo.chip(c))
    if rank is None and core not in helpers + takers:
        return
    sent = [0]
    mine = topo.chip(core)
    OFF = 0
    ALL = 0
    for c in cores + helpers + takers:
        if topo.chip(c) != mine:
            OFF = topo.mask(core, c)
        elif c != core:
            ALL = topo.mask(core, c)
    BULK = ALL & ~OFF

    def ids(dsts):
        out = []
        for d in dsts:
            rid, pid, _s = topo.addr(d)
            out.append(DstId(rid=rid, pnc=pid))
        return out

    def send(dsts, sc, ss, dc, ds, sem, mask):
        for a, b in ((sc.bitcast(dt.uint8), dc.bitcast(dt.uint8)), (ss, ds)):
            if len(dsts) == 1:
                rid, pid, _s = topo.addr(dsts[0])
                g.remote_dma(b, a, sem, T.sem.sent, pid, rid, mask)
            else:
                g.remote_dma_fused([RemoteDMATransfer(dst_ids=ids(dsts), dma_engine_mask=mask, remote_sem=sem,
                                                      srcs=[a], dsts=[b for _ in dsts])], local_sem=T.sem.sent)
            sent[0] += bits(mask)

    def send_h(j, dsts, mask):
        a, b = 256 * j, 256 * j + 256
        send(dsts, T.hc[:, a:b], T.hs[:, a:b], T.hc[:, a:b], T.hs[:, a:b], T.sem["ah%d" % j], mask)

    if rank is None:
        i = chips.index(mine)
        nc = len(chips)

        def at_chip(k):
            for j, c in enumerate(cores):
                if topo.chip(c) == chips[k] and topo.die(c) == topo.die(core):
                    return j
        here = [c for c in cores if topo.chip(c) == mine]
        own = at_chip(i)
        g.wait_ge(T.sem["ah%d" % own], 2 * bits(BULK))
        if core in helpers:
            for p in range(1, nc):
                send_h(own, [takers[at_chip((i + p) % nc)]], OFF)
        else:
            send_h(own, [c for c in here if c != cores[own]], ALL)
            for p in range(1, nc):
                j = at_chip((i - p) % nc)
                g.wait_ge(T.sem["ah%d" % j], 2 * bits(OFF))
                send_h(j, here, ALL)
        g.wait_ge(T.sem.sent, sent[0])
        return

    last = rank == N - 1
    V, S, P, Y = g.vector, g.scalar, g.tensor, g.sync
    RELU, COPY = ActivationFunctionType.Relu, ActivationFunctionType.Copy
    hs0 = 256 * rank

    if last:
        for p in range(4):
            o = 1024 * (p % 2) + 512 * (p // 2)
            Y.dma_start(T.pxt[:, 512 * p:512 * p + 512], T.px[:, o:o + 512]).then_inc(T.sem["ld_p%d" % p], 16)
        Y.dma_start(T.xt[:], T.x[:]).then_inc(T.sem.ld_x, 16)
        Y.dma_start(T.w1t[:], T.w1[:]).then_inc(T.sem.ld_w1, 16)
        Y.wait_ge(T.sem.q_h, 1)
        Y.dma_start(T.w2t[:], T.w2[:]).then_inc(T.sem.ld_w2, 16)
        Y.dma_start(T.pwt[:], T.pw[:]).then_inc(T.sem.ld_pw, 16)
    else:
        Y.dma_start(T.pwt[:], T.pw[:]).then_inc(T.sem.ld_pw, 16)
        Y.dma_start(T.xt[:], T.x[:]).then_inc(T.sem.ld_x, 16)
        Y.dma_start(T.w1t[:], T.w1[:]).then_inc(T.sem.ld_w1, 16)
        Y.dma_start(T.w2t[:], T.w2[:]).then_inc(T.sem.ld_w2, 16)

    def quant_pw():
        k = slot_of(rank, rank)
        V.wait_ge(T.sem.ld_pw, 16)
        V.quantize_mx(T.wc[:, 256 * k:256 * k + 256], T.ws[:, 256 * k:256 * k + 256], T.pwt[:]).then_inc(T.sem.q_pw, 1)

    def acts(z0, z1, t, a, n, s0, s1, done):
        S.wait_ge(s0, 1)
        S.activation(t[:, a:a + 4 * n:4], z0, RELU, scale=CC).then_inc(done, 1)
        S.activation(t[:, a + 1:a + 4 * n:4], z0, RELU, scale=-CC).then_inc(done, 1)
        V.wait_ge(s1, 1)
        V.tensor_scalar(t[:, a + 2:a + 4 * n:4], z1, CC, 0.0, AluOpType.mult, AluOpType.max).then_inc(done, 1)
        V.tensor_scalar(t[:, a + 3:a + 4 * n:4], z1, -CC, 0.0, AluOpType.mult, AluOpType.max).then_inc(done, 1)
        V.wait_ge(done, 4)

    if last:
        for p in range(4):
            V.wait_ge(T.sem["ld_p%d" % p], 16)
            c = slice(PW_ * p, PW_ * p + PW_)
            V.quantize_mx(T.pxc[:, c], T.pxs[:, c], T.pxt[:, 512 * p:512 * p + 512]).then_inc(T.sem["q_p%d" % p], 1)
            g.wait_ge(T.sem["q_p%d" % p], 1)
            send([cores[RUNS[p][0][0]]], T.pxc[:, c], T.pxs[:, c], T.lc[:, c], T.ls[:, c], T.sem["ap%d" % p], OFF)
    else:
        quant_pw()
        k = 256 * slot_of(rank, rank)
        k2 = 256 * (rank % 3)
        g.wait_ge(T.sem.q_pw, 1)
        dsts = [cores[r] for r in range(N) if r != rank and needs(r, rank)]
        send(dsts, T.wc[:, k:k + 256], T.ws[:, k:k + 256], T.wc[:, k2:k2 + 256], T.ws[:, k2:k2 + 256], T.sem["aw%d" % rank], OFF)

    V.wait_ge(T.sem.ld_x, 16)
    V.quantize_mx(T.xc[:], T.xs[:], T.xt[:]).then_inc(T.sem.q_x, 1)
    V.wait_ge(T.sem.ld_w1, 16)
    V.quantize_mx(T.w1c[:], T.w1s[:], T.w1t[:]).then_inc(T.sem.q_w1, 1)
    P.wait_ge(T.sem.q_x, 1)
    P.wait_ge(T.sem.q_w1, 1)
    zh = [T.py[:, 0:256], T.py[:, 512:768]]
    for i in range(2):
        P.matmul_mx(zh[i], T.w1c[:, 128 * i:128 * i + 128], T.w1s[:, 128 * i:128 * i + 128], T.xc[:], T.xs[:],
                    True, True).then_inc(T.sem["zh%d" % i], 1)
    acts(zh[0], zh[1], T.ht, 0, 256, T.sem.zh0, T.sem.zh1, T.sem.act_h)
    V.quantize_mx(T.hc[:, hs0:hs0 + 256], T.hs[:, hs0:hs0 + 256], T.ht[:]).then_inc(T.sem.q_h, 1)
    g.wait_ge(T.sem.q_h, 1)
    send_h(rank, [helpers[rank], takers[rank]], BULK)
    V.wait_ge(T.sem.ld_w2, 16)
    V.quantize_mx(T.w2c[:], T.w2s[:], T.w2t[:]).then_inc(T.sem.q_w2, 1)
    if last:
        quant_pw()

    P.wait_ge(T.sem.q_h, 1)
    P.wait_ge(T.sem.q_w2, 1)
    ci = chips.index(mine)
    order = [chips[(ci - p) % len(chips)] for p in range(len(chips))]

    def y_group(q):
        js = [j for j in range(N) if topo.chip(cores[j]) == order[q]]
        a = 256 * js[0]
        b = (2 + q) % 4
        for j in js:
            if j != rank:
                P.wait_ge(T.sem["ah%d" % j], 2 * bits(ALL))
        if q == 4:
            P.wait_ge(T.sem.cy0, 1)
        bank = T.py[:, 512 * b:512 * b + 512]
        P.matmul_mx(bank, T.w2c[:], T.w2s[:], T.hc[:, a:a + 512], T.hs[:, a:a + 512], True, True).then_inc(T.sem["my%d" % q], 1)
        if q % 2 == 0:
            S.wait_ge(T.sem["my%d" % q], 1)
            S.activation(T.ysb[:, a:a + 512], bank, COPY).then_inc(T.sem["cy%d" % q], 1)
        else:
            V.wait_ge(T.sem["my%d" % q], 1)
            V.tensor_copy(T.ysb[:, a:a + 512], bank).then_inc(T.sem["cy%d" % q], 1)
        Y.wait_ge(T.sem["cy%d" % q], 1)
        Y.dma_start(T.y[:, a:a + 512], T.ysb[:, a:a + 512]).then_inc(T.sem.sty, 16)

    for q in range(EARLY[rank]):
        y_group(q)

    n = [0]

    def layer(s, mc, ms, wait, wn):
        k = n[0]
        sl = slot_of(rank, s)
        if s == rank:
            P.wait_ge(T.sem.q_pw, 1)
        else:
            P.wait_ge(T.sem["aw%d" % s], 2 * bits(OFF))
        P.wait_ge(wait, wn)
        out = []
        for i in range(2):
            b = 2 * (k % 2) + i
            z = T.pc[:, 512 * b:512 * b + PW_]
            w = slice(256 * sl + 128 * i, 256 * sl + 128 * i + 128)
            P.matmul_mx(z, T.wc[:, w], T.ws[:, w], mc, ms, True, True).then_inc(T.sem["z%d_%d" % (i, k)], 1)
            out.append(z)
        n[0] += 1
        return k, out

    for p in ORDER[rank]:
        c = slice(PW_ * p, PW_ * p + PW_)
        path = [N - 1] + [r for r, _a, _b in RUNS[p]] + [N - 1]
        at = len(path) - 1 if last else path.index(rank, 1)
        mc, ms, wait, wn = T.lc[:, c], T.ls[:, c], T.sem["ap%d" % p], 2 * bits(topo.mask(cores[path[at - 1]], core))
        if last:
            if n[0] >= 2:
                for i in range(2):
                    P.wait_ge(T.sem["zc%d_%d" % (ORDER[rank][n[0] - 2], i)], 1)
            k, Z = layer(N - 1, mc, ms, wait, wn)
            for i in range(2):
                o = 256 * (2 * (p % 2) + i) + PW_ * (p // 2)
                zs = T.zsb[:, o:o + PW_]
                done = T.sem["zc%d_%d" % (p, i)]
                if i == 0:
                    S.wait_ge(T.sem["z0_%d" % k], 1)
                    S.activation(zs, Z[0], COPY).then_inc(done, 1)
                else:
                    V.wait_ge(T.sem["z1_%d" % k], 1)
                    V.tensor_copy(zs, Z[1]).then_inc(done, 1)
                Q = S if i == 0 else Y
                Q.wait_ge(done, 1)
                Q.dma_start(T.z[:, o:o + PW_], zs).then_inc(T.sem.stz, 16)
            continue
        _r, s0, s1 = RUNS[p][at - 1]
        for s in range(s0, s1 + 1):
            k, Z = layer(s, mc, ms, wait, wn)
            acts(Z[0], Z[1], T.ct, 512 * k, PW_, T.sem["z0_%d" % k], T.sem["z1_%d" % k], T.sem["act%d" % k])
            o = slice(PW_ * k, PW_ * k + PW_)
            mc, ms, wait, wn = T.cc[:, o], T.cs[:, o], T.sem["q%d" % k], 1
            V.quantize_mx(mc, ms, T.ct[:, 512 * k:512 * k + 512]).then_inc(wait, 1)
        dst = cores[path[at + 1]]
        g.wait_ge(wait, 1)
        send([dst], mc, ms, T.lc[:, c], T.ls[:, c], T.sem["ap%d" % p], topo.mask(core, dst))

    if not last:
        Y.wait_ge(T.sem.sent, sent[0])
    for q in range(EARLY[rank], 5):
        y_group(q)

    Y.wait_ge(T.sem.sty, 80)
    if last:
        Y.wait_ge(T.sem.stz, 128)
    g.wait_ge(T.sem.sent, sent[0])
